import numpy as np
CORES = [0,1,2,3]
N = 4
def setup_inputs(rng):
    return {"x1": rng.standard_normal((N, 128, 16), dtype=np.float32), "x2": rng.standard_normal((N, 128, 1), dtype=np.float32), "x3": rng.standard_normal((N, 128, 64), dtype=np.float32), "x4": rng.standard_normal((N, 128, 4), dtype=np.float32)}
def reference(x1, x2, x3, x4):
    out = {}
    s = x1.sum(axis=0, dtype=np.float64).astype(x1.dtype)
    out["y1"] = np.broadcast_to(s, (N,) + s.shape)
    s = x2.sum(axis=0, dtype=np.float64).astype(x2.dtype)
    out["y2"] = np.broadcast_to(s, (N,) + s.shape)
    s = x3.sum(axis=0, dtype=np.float64).astype(x3.dtype)
    out["y3"] = np.broadcast_to(s, (N,) + s.shape)
    s = x4.sum(axis=0, dtype=np.float64).astype(x4.dtype)
    out["y4"] = np.broadcast_to(s, (N,) + s.shape)
    return out

@@ -1,0 +1,58 @@
+from concourse.bass import DstId, RemoteDMATransfer
+
+WIDTHS = [16, 1, 64, 4]
+OFFS = [0, 16, 17, 81]
+W = 85
+HELPER = 4
+
+SCRATCH = {
+    "pack": ("sbuf", [128, W], "float32"),
+    "land": ("sbuf", [128, 4 * W], "float32"),
+    "res": ("sbuf", [128, W], "float32"),
+}
+SEMAPHORES = ["loaded", "sent", "arrived", "summed", "stored"]
+
+
+def rank_program(g, core, T, topo):
+    rank = T.rank_of(core)
+    if core == HELPER:
+        g.wait_ge(T.sem.arrived, 16 * len(T.cores))
+        ids = []
+        for c in T.cores:
+            rid, pid, _se = topo.addr(c)
+            ids.append(DstId(rid=rid, pnc=pid))
+        g.remote_dma_fused(
+            [RemoteDMATransfer(
+                dst_ids=ids,
+                dma_engine_mask=0xFFFF,
+                remote_sem=T.sem.summed,
+                srcs=[T.land[:, r * W:(r + 1) * W] for r in range(len(T.cores))],
+                dsts=[T.res[:] for _c in T.cores],
+                alu_op=1,
+            )],
+            local_sem=T.sem.sent,
+        )
+        g.wait_ge(T.sem.sent, 16)
+        return
+    if rank is None:
+        return
+
+    xs = [T.x1, T.x2, T.x3, T.x4]
+    ys = [T.y1, T.y2, T.y3, T.y4]
+    queues = [g.sync, g.scalar, g.scalar, g.sync]
+
+    for q, x, o, w in zip(queues, xs, OFFS, WIDTHS):
+        q.dma_start(T.pack[:, o:o + w], x[:]).then_inc(T.sem.loaded, 16)
+    g.wait_ge(T.sem.loaded, 64)
+
+    rid, pid, _se = topo.addr(HELPER)
+    g.remote_dma(T.land[:, rank * W:(rank + 1) * W], T.pack[:], T.sem.arrived, T.sem.sent, pid, rid,
+                 topo.mask(core, HELPER))
+
+    g.sync.wait_ge(T.sem.summed, 16)
+    g.scalar.wait_ge(T.sem.summed, 16)
+    for q, y, o, w in zip(queues, ys, OFFS, WIDTHS):
+        q.dma_start(y[:], T.res[:, o:o + w]).then_inc(T.sem.stored, 16)
+    g.wait_ge(T.sem.sent, 16)
+    g.wait_ge(T.sem.summed, 16)
+    g.wait_ge(T.sem.stored, 64)

@@ -1,58 +1,76 @@
 from concourse.bass import DstId, RemoteDMATransfer
 
-WIDTHS = [16, 1, 64, 4]
-OFFS = [0, 16, 17, 81]
-W = 85
-HELPER = 4
+SLOTS = 3
+HELPERS = [4, 5, 6]
+SLOT_MASKS = [0x000F, 0x00F0, 0x0F00]
+ENG = 4
 
 SCRATCH = {
-    "pack": ("sbuf", [128, W], "float32"),
-    "land": ("sbuf", [128, 4 * W], "float32"),
-    "res": ("sbuf", [128, W], "float32"),
+    "pack": ("dram", [SLOTS, 128, 32], "float32"),
+    "land": ("dram", [4, 128, 32], "float32"),
+    "res": ("dram", [SLOTS, 128, 32], "float32"),
 }
-SEMAPHORES = ["loaded", "sent", "arrived", "summed", "stored"]
+SEMAPHORES = ["loaded", "filled", "sent", "arrived", "summed", "stored"]
+
+
+def dst_id(topo, c):
+    rid, pid, _se = topo.addr(c)
+    return DstId(rid=rid, pnc=pid)
+
+
+def pieces(buf):
+    return [buf[2, 0:64, :], buf[2, 80:84, :], buf[0:2], buf[2, 64:80, :]]
 
 
 def rank_program(g, core, T, topo):
-    rank = T.rank_of(core)
-    if core == HELPER:
-        g.wait_ge(T.sem.arrived, 16 * len(T.cores))
-        ids = []
-        for c in T.cores:
-            rid, pid, _se = topo.addr(c)
-            ids.append(DstId(rid=rid, pnc=pid))
+    n = len(T.cores)
+    if core in HELPERS:
+        k = HELPERS.index(core)
+        g.wait_ge(T.sem.arrived, ENG * n)
         g.remote_dma_fused(
             [RemoteDMATransfer(
-                dst_ids=ids,
+                dst_ids=[dst_id(topo, c) for c in T.cores],
                 dma_engine_mask=0xFFFF,
                 remote_sem=T.sem.summed,
-                srcs=[T.land[:, r * W:(r + 1) * W] for r in range(len(T.cores))],
-                dsts=[T.res[:] for _c in T.cores],
+                srcs=[T.land[r] for r in range(n)],
+                dsts=[T.res[k] for _c in T.cores],
                 alu_op=1,
             )],
             local_sem=T.sem.sent,
         )
         g.wait_ge(T.sem.sent, 16)
         return
+
+    rank = T.rank_of(core)
     if rank is None:
         return
 
     xs = [T.x1, T.x2, T.x3, T.x4]
     ys = [T.y1, T.y2, T.y3, T.y4]
-    queues = [g.sync, g.scalar, g.scalar, g.sync]
+    queues = [g.scalar, g.sync, g.sync, g.scalar]
 
-    for q, x, o, w in zip(queues, xs, OFFS, WIDTHS):
-        q.dma_start(T.pack[:, o:o + w], x[:]).then_inc(T.sem.loaded, 16)
+    for q, x, p in zip(queues, xs, pieces(T.pack)):
+        q.dma_start(p, x[:]).then_inc(T.sem.loaded, 16)
+    g.dma_start(T.pack[2, 84:128, :], T.x1[0:88, :]).then_inc(T.sem.filled, 16)
+    g.wait_ge(T.sem.filled, 16)
     g.wait_ge(T.sem.loaded, 64)
 
-    rid, pid, _se = topo.addr(HELPER)
-    g.remote_dma(T.land[:, rank * W:(rank + 1) * W], T.pack[:], T.sem.arrived, T.sem.sent, pid, rid,
-                 topo.mask(core, HELPER))
+    g.remote_dma_fused(
+        [RemoteDMATransfer(
+            dst_ids=[dst_id(topo, HELPERS[k])],
+            dma_engine_mask=SLOT_MASKS[k],
+            remote_sem=T.sem.arrived,
+            src=T.pack[k],
+            dst=T.land[rank],
+        ) for k in range(SLOTS)],
+        local_sem=T.sem.sent,
+    )
 
-    g.sync.wait_ge(T.sem.summed, 16)
-    g.scalar.wait_ge(T.sem.summed, 16)
-    for q, y, o, w in zip(queues, ys, OFFS, WIDTHS):
-        q.dma_start(y[:], T.res[:, o:o + w]).then_inc(T.sem.stored, 16)
-    g.wait_ge(T.sem.sent, 16)
-    g.wait_ge(T.sem.summed, 16)
+    g.sync.wait_ge(T.sem.summed, 16 * SLOTS)
+    g.scalar.wait_ge(T.sem.summed, 16 * SLOTS)
+    for q, y, p in zip(queues, ys, pieces(T.res)):
+        q.dma_start(y[:], p).then_inc(T.sem.stored, 16)
+
+    g.wait_ge(T.sem.sent, ENG * SLOTS)
+    g.wait_ge(T.sem.summed, 16 * SLOTS)
     g.wait_ge(T.sem.stored, 64)

from concourse.bass import DstId, RemoteDMATransfer

SLOTS = 3
HELPERS = [4, 5, 6]
SLOT_MASKS = [0x000F, 0x00F0, 0x0F00]
ENG = 4

SCRATCH = {
    "pack": ("dram", [SLOTS, 128, 32], "float32"),
    "land": ("dram", [4, 128, 32], "float32"),
    "res": ("dram", [SLOTS, 128, 32], "float32"),
}
SEMAPHORES = ["loaded", "filled", "sent", "arrived", "summed", "stored"]


def dst_id(topo, c):
    rid, pid, _se = topo.addr(c)
    return DstId(rid=rid, pnc=pid)


def pieces(buf):
    return [buf[2, 0:64, :], buf[2, 80:84, :], buf[0:2], buf[2, 64:80, :]]


def rank_program(g, core, T, topo):
    n = len(T.cores)
    if core in HELPERS:
        k = HELPERS.index(core)
        g.wait_ge(T.sem.arrived, ENG * n)
        g.remote_dma_fused(
            [RemoteDMATransfer(
                dst_ids=[dst_id(topo, c) for c in T.cores],
                dma_engine_mask=0xFFFF,
                remote_sem=T.sem.summed,
                srcs=[T.land[r] for r in range(n)],
                dsts=[T.res[k] for _c in T.cores],
                alu_op=1,
            )],
            local_sem=T.sem.sent,
        )
        g.wait_ge(T.sem.sent, 16)
        return

    rank = T.rank_of(core)
    if rank is None:
        return

    xs = [T.x1, T.x2, T.x3, T.x4]
    ys = [T.y1, T.y2, T.y3, T.y4]
    queues = [g.scalar, g.sync, g.sync, g.scalar]

    for q, x, p in zip(queues, xs, pieces(T.pack)):
        q.dma_start(p, x[:]).then_inc(T.sem.loaded, 16)
    g.dma_start(T.pack[2, 84:128, :], T.x1[0:88, :]).then_inc(T.sem.filled, 16)
    g.wait_ge(T.sem.filled, 16)
    g.wait_ge(T.sem.loaded, 64)

    g.remote_dma_fused(
        [RemoteDMATransfer(
            dst_ids=[dst_id(topo, HELPERS[k])],
            dma_engine_mask=SLOT_MASKS[k],
            remote_sem=T.sem.arrived,
            src=T.pack[k],
            dst=T.land[rank],
        ) for k in range(SLOTS)],
        local_sem=T.sem.sent,
    )

    g.sync.wait_ge(T.sem.summed, 16 * SLOTS)
    g.scalar.wait_ge(T.sem.summed, 16 * SLOTS)
    for q, y, p in zip(queues, ys, pieces(T.res)):
        q.dma_start(y[:], p).then_inc(T.sem.stored, 16)

    g.wait_ge(T.sem.sent, ENG * SLOTS)
    g.wait_ge(T.sem.summed, 16 * SLOTS)
    g.wait_ge(T.sem.stored, 64)
